import numpy as np, ml_dtypes
CORES = [6,14,22,30,38,46,54,62,70,78,86,94,102,110,118,126,196,197,198,199]
N = 20
TOK = 32
EXPERTS = [3,8,9,10,13,19]
ROUTE = [[[3,9],[9,10],[9,13],[8,10],[8,13],[3,9],[3,9],[3,13],[3,9],[9,10],[10,19],[3,10],[9,10],[8,13],[3,8],[9,13],[3,8],[3,8],[9,19],[8,13],[3,8],[3,8],[3,19],[10,19],[8,9],[8,13],[9,13],[3,13],[10,13],[10,13],[13,19],[9,13]],[[3,9],[8,9],[3,19],[8,13],[3,19],[8,10],[8,13],[3,8],[9,10],[3,10],[3,8],[8,13],[13,19],[8,10],[3,10],[10,13],[8,13],[8,19],[9,10],[9,19],[10,13],[3,9],[9,19],[9,10],[9,19],[10,19],[8,10],[3,13],[8,13],[8,13],[3,13],[3,9]],[[3,19],[3,13],[9,10],[8,10],[10,19],[3,9],[8,10],[8,19],[10,13],[8,13],[3,9],[10,13],[9,13],[8,13],[10,13],[13,19],[3,10],[8,19],[8,19],[10,19],[3,13],[9,13],[10,19],[10,19],[8,13],[8,9],[9,19],[9,13],[8,9],[9,19],[3,9],[13,19]],[[3,13],[3,13],[9,19],[13,19],[8,9],[8,9],[9,13],[9,13],[8,9],[8,13],[3,13],[13,19],[13,19],[8,9],[3,8],[13,19],[8,13],[8,10],[3,19],[3,13],[9,13],[10,13],[8,19],[10,19],[3,19],[9,10],[10,13],[3,8],[9,10],[8,10],[9,10],[3,13]],[[10,19],[3,10],[3,8],[8,10],[3,8],[3,10],[8,9],[13,19],[8,10],[8,9],[9,10],[8,10],[9,10],[3,13],[8,10],[13,19],[13,19],[8,19],[8,9],[8,10],[8,9],[10,19],[3,9],[13,19],[3,9],[10,13],[9,19],[9,10],[3,9],[9,19],[8,13],[8,10]],[[3,19],[10,13],[8,10],[9,19],[13,19],[9,19],[8,10],[8,13],[9,19],[9,10],[8,13],[13,19],[3,13],[3,10],[9,10],[8,9],[8,9],[8,9],[8,13],[3,19],[8,10],[3,10],[10,13],[8,10],[8,13],[8,19],[8,10],[8,13],[9,19],[9,19],[3,9],[10,19]],[[9,13],[13,19],[3,19],[3,19],[3,8],[3,9],[3,9],[8,9],[13,19],[9,13],[10,19],[8,10],[9,13],[9,13],[8,19],[8,19],[10,13],[9,19],[3,19],[10,13],[8,10],[10,13],[8,13],[8,10],[9,19],[3,10],[9,19],[8,9],[10,19],[8,19],[3,8],[3,13]],[[3,13],[3,8],[3,19],[3,9],[8,10],[3,9],[3,13],[3,19],[3,13],[9,10],[8,19],[3,10],[3,8],[3,19],[9,13],[9,19],[3,19],[3,19],[8,13],[3,10],[13,19],[10,13],[3,9],[9,13],[9,19],[8,9],[8,13],[8,10],[3,10],[10,13],[10,13],[10,19]],[[3,19],[10,19],[8,10],[3,8],[9,10],[10,13],[8,19],[13,19],[9,13],[8,9],[8,13],[3,10],[3,19],[8,19],[9,10],[3,10],[10,13],[3,8],[9,13],[8,9],[3,10],[9,19],[9,10],[10,19],[3,13],[9,13],[8,10],[8,9],[10,19],[13,19],[8,9],[3,9]],[[8,13],[13,19],[3,9],[9,10],[3,8],[3,13],[9,19],[3,8],[10,19],[13,19],[9,13],[8,19],[9,10],[9,19],[8,10],[3,19],[8,19],[8,10],[8,19],[10,19],[9,19],[8,9],[3,10],[3,8],[8,13],[13,19],[10,13],[3,9],[3,8],[8,19],[8,9],[10,13]],[[9,13],[8,10],[9,19],[13,19],[9,13],[8,19],[3,19],[8,9],[13,19],[3,10],[3,8],[10,19],[9,19],[9,10],[8,9],[10,19],[3,13],[9,10],[8,19],[9,13],[8,9],[3,9],[9,10],[3,8],[3,13],[10,13],[3,19],[10,13],[8,13],[3,9],[3,13],[10,19]],[[10,19],[3,9],[8,13],[9,10],[3,19],[10,19],[8,13],[9,19],[3,9],[9,13],[8,9],[13,19],[8,10],[3,13],[3,13],[10,13],[3,9],[8,13],[3,9],[3,19],[3,19],[3,8],[3,9],[10,19],[3,8],[10,19],[8,19],[3,19],[3,8],[9,19],[3,19],[9,10]],[[3,13],[8,19],[8,13],[9,13],[8,10],[8,10],[10,19],[3,9],[9,19],[9,19],[3,13],[10,19],[8,19],[10,19],[8,10],[8,9],[9,13],[9,10],[10,19],[3,9],[9,13],[9,19],[9,13],[8,9],[3,19],[8,9],[9,19],[13,19],[8,19],[3,10],[9,13],[13,19]],[[3,10],[13,19],[10,13],[9,19],[3,13],[3,9],[3,8],[3,19],[8,19],[3,9],[10,19],[8,10],[3,10],[8,19],[8,19],[8,13],[8,19],[3,10],[10,13],[3,19],[13,19],[8,10],[9,19],[10,13],[3,9],[8,10],[9,13],[10,13],[10,13],[8,10],[9,13],[8,13]],[[8,10],[13,19],[8,19],[3,10],[3,10],[3,8],[9,19],[9,10],[8,13],[3,10],[9,10],[13,19],[10,19],[9,10],[13,19],[9,13],[10,19],[9,19],[9,13],[3,19],[8,9],[9,19],[3,19],[8,19],[3,9],[9,10],[10,19],[9,10],[3,8],[13,19],[9,19],[8,9]],[[8,13],[9,13],[3,13],[13,19],[13,19],[3,8],[9,10],[8,13],[9,19],[9,13],[3,19],[3,10],[8,13],[3,9],[13,19],[8,13],[9,13],[8,13],[9,19],[10,13],[8,19],[10,13],[8,10],[3,8],[3,19],[3,19],[8,13],[8,19],[3,10],[3,10],[9,10],[3,10]],[[10,13],[3,19],[8,19],[9,10],[3,9],[8,9],[8,9],[9,10],[3,10],[9,10],[3,19],[9,13],[3,10],[9,19],[9,10],[3,13],[10,13],[8,9],[3,9],[3,13],[13,19],[3,9],[3,10],[3,19],[3,10],[13,19],[13,19],[3,9],[3,10],[13,19],[13,19],[3,9]],[[8,10],[9,19],[3,10],[3,10],[8,10],[13,19],[10,13],[9,13],[3,10],[10,13],[10,13],[3,10],[9,19],[3,9],[9,19],[8,13],[3,9],[3,13],[8,9],[10,19],[10,19],[3,10],[3,19],[3,8],[9,13],[3,13],[3,8],[3,13],[3,10],[13,19],[9,10],[3,13]],[[10,13],[3,13],[3,10],[3,13],[3,10],[9,13],[8,10],[9,19],[8,13],[9,10],[3,9],[3,8],[8,10],[8,9],[8,13],[3,19],[9,19],[8,13],[8,19],[3,9],[8,13],[8,19],[9,19],[3,9],[8,13],[3,13],[3,9],[8,13],[8,13],[13,19],[8,19],[3,10]],[[8,13],[8,10],[3,19],[3,9],[13,19],[9,13],[3,10],[13,19],[9,13],[3,10],[8,9],[3,13],[8,10],[9,19],[3,10],[8,13],[10,13],[9,19],[3,19],[9,10],[10,13],[3,13],[8,19],[10,19],[10,19],[9,10],[3,9],[3,13],[8,19],[9,13],[8,9],[8,10]]]
def setup_inputs(rng):
    return {"x": rng.standard_normal((N, 128, TOK), dtype=np.float32).astype(ml_dtypes.bfloat16), "w": rng.standard_normal((N, 128, 128), dtype=np.float32).astype(ml_dtypes.bfloat16)}
def reference(x, w):
    X, W = x.astype(np.float64), w.astype(np.float64)
    y = np.zeros((N, 128, TOK))
    for r in range(N):
        for t in range(TOK):
            for e in ROUTE[r][t]:
                y[r][:, t] += W[e].T @ X[r][:, t]
    return {"y": y.astype(ml_dtypes.bfloat16 if x.dtype != np.float64 else np.float64)}

@@ -1,0 +1,194 @@
+from concourse.bass import DstId, RemoteDMATransfer
+from concourse.mybir import dt, AluOpType
+import comms_topo
+
+SCRATCH = {
+    "wd": ("dram", [2, 128, 128], "bfloat16"),
+    "wsb": ("sbuf", [128, 768], "bfloat16"),
+    "xsb": ("sbuf", [128, 32], "bfloat16"),
+    "mask": ("sbuf", [128, 192], "bfloat16"),
+    "xm": ("sbuf", [128, 192], "bfloat16"),
+    "ysb": ("sbuf", [128, 32], "bfloat16"),
+    "ps": ("psum", [128, 32], "float32"),
+}
+SEMAPHORES = ["ld", "xl", "rl0", "rl1", "w0", "w1", "w2", "w3", "w4", "w5", "snt", "vs", "vm", "mm", "cp", "st"]
+
+INBOUND = {3: (202, 0), 13: (206, 0), 8: (195, 0), 10: (197, 1), 9: (199, 0)}
+FAR = {}
+_CACHE = {}
+
+
+def _nbits(m):
+    return bin(m).count("1")
+
+
+def build_plan(cores, experts):
+    topo = comms_topo
+    jobs, selfload, expect = {}, {}, {}
+    inport = {}
+    big = [c for c in cores if topo.host(c) == 1]
+
+    def place(c):
+        return (topo.host(c), topo.chip(c))
+
+    for k, e in enumerate(experts):
+        root = cores[e]
+        base = root - root % 8
+        par = topo.chip(root) % 2
+        on_big = root in big
+        own = 1 if on_big else 0
+        wk = "w%d" % k
+        far = FAR.get(e, [])
+        covered = [c for _, ds in far for c in ds]
+        singles = [c for c in cores if c not in big and c != root and c not in covered]
+        same = [c for c in singles if topo.chip(c) % 2 == par]
+        cross = [c for c in singles if topo.chip(c) % 2 != par]
+        if on_big:
+            caps_same = {1: [(base + 0, 3), (base + 1, 2)], 0: [(base + 4, 3)]}
+            caps_cross = {1: [(base + 2, 3)], 0: [(base + 6, 3), (root, 2)]}
+        elif far:
+            caps_same = {1: [(base + 0, 2), (base + 1, 2)], 0: [(base + 4, 2), (base + 5, 2)]}
+            caps_cross = {1: [(base + 2, 2), (base + 3, 2)], 0: [(base + 7, 2)]}
+        else:
+            caps_same = {1: [(base + 0, 2), (base + 1, 2)], 0: [(base + 4, 2), (base + 5, 2)]}
+            caps_cross = {1: [(base + 2, 2), (base + 3, 2)], 0: [(base + 7, 2), (root, 2)]}
+        send = {}
+        for dests, caps in ((same, caps_same), (cross, caps_cross)):
+            cap1 = sum(n for _, n in caps[1])
+            n1 = cap1 if on_big else min(cap1, (len(dests) + 1) // 2)
+            order = sorted(dests, key=lambda c: (inport.get((place(c), 1), 0) - inport.get((place(c), 0), 0), c))
+            for d, part in ((1, order[:n1]), (0, order[n1:])):
+                names = [s for s, _ in caps[d]]
+                left = dict(caps[d])
+                i = 0
+                for c in part:
+                    while left[names[i % len(names)]] == 0:
+                        i += 1
+                    s = names[i % len(names)]
+                    left[s] -= 1
+                    i += 1
+                    send.setdefault(s, []).append(c)
+                    inport[(place(c), d)] = inport.get((place(c), d), 0) + 1
+        tr = []
+        helpers = [s for s in send if s != root]
+        if on_big:
+            helpers = sorted(set(helpers) | set(c for c in big if c != root))
+        tr.append((0xFF00, "rl0", ("d", own), ("d", 0), sorted(helpers)))
+        direct = send.get(root, [])
+        bmask, dmask = (0x000F, 0x00F0) if direct and not on_big else (0x00FF, 0x00FF)
+        if not on_big:
+            rc, slot = INBOUND[e]
+            away = [rc] + [f for f, _ in far]
+            tr.append((bmask, "rl%d" % slot, ("d", own), ("d", slot), away))
+            targets = [c for c in big if c != rc]
+            m = 0xFFFF if place(rc) == place(big[0]) else 0x00FF
+            jobs.setdefault(rc, []).append((("rl%d" % slot, _nbits(bmask)), [(m, wk, ("d", slot), ("s", k), targets)]))
+            for c in targets:
+                expect.setdefault(c, {})[k] = _nbits(m)
+            if rc in big:
+                selfload.setdefault(rc, []).append((slot, _nbits(bmask), k))
+                expect.setdefault(rc, {})[k] = 16
+            for f, ds in far:
+                near = [c for c in ds if place(c) == place(f)]
+                off = [c for c in ds if place(c) != place(f)]
+                ftr = [(0x00FF, wk, ("d", slot), ("s", k), off)]
+                if near:
+                    ftr.append((0xFF00, wk, ("d", slot), ("s", k), near))
+                jobs.setdefault(f, []).append((("rl%d" % slot, _nbits(bmask)), ftr))
+                for c in ds:
+                    expect.setdefault(c, {})[k] = 8
+                    if place(c) != place(f):
+                        inport[(place(c), topo.die(f))] = inport.get((place(c), topo.die(f)), 0) + 1
+        if direct:
+            tr.append((dmask, wk, ("d", own), ("s", k), direct))
+        for c in direct:
+            expect.setdefault(c, {})[k] = _nbits(dmask)
+        jobs.setdefault(root, []).insert(0, (("ld", 16), tr))
+        expect.setdefault(root, {})[k] = 16
+        for s in helpers:
+            if s in send:
+                jobs.setdefault(s, []).insert(0, (("rl0", 8), [(0x00FF, wk, ("d", 0), ("s", k), send[s])]))
+                for c in send[s]:
+                    expect.setdefault(c, {})[k] = 8
+            if s in big:
+                selfload.setdefault(s, []).append((0, 8, k))
+                expect.setdefault(s, {})[k] = 16
+    return jobs, selfload, expect
+
+
+def rank_program(g, core, T, topo):
+    cores = list(T.cores)
+    experts = list(T.tables["EXPERTS"])
+    route = T.tables["ROUTE"]
+    tok = T.tables["TOK"]
+    if "p" not in _CACHE:
+        _CACHE["p"] = build_plan(cores, experts)
+    jobs, selfload, expect = _CACHE["p"]
+    rank = T.rank_of(core)
+    is_root = rank is not None and rank in experts
+
+    def ap(where):
+        kind, i = where
+        return T.wd[i] if kind == "d" else T.wsb[:, i * 128:(i + 1) * 128]
+
+    if is_root:
+        k_own = experts.index(rank)
+        g.sync.dma_start(T.wd[1 if topo.host(core) == 1 else 0], T.w[:]).then_inc(T.sem.ld, 16)
+    if rank is not None:
+        g.scalar.dma_start(T.xsb[:], T.x[:]).then_inc(T.sem.xl, 16)
+    if is_root:
+        g.scalar.dma_start(ap(("s", k_own)), T.w[:]).then_inc(T.sem["w%d" % k_own], 16)
+
+    sent = 0
+    for wait, transfers in jobs.get(core, []):
+        g.wait_ge(T.sem[wait[0]], wait[1])
+        trs = []
+        for mask, rsem, src, dst, dests in transfers:
+            ids = []
+            for d in dests:
+                rid, pid = topo.addr(d, core)
+                ids.append(DstId(rid=rid, pnc=pid))
+            trs.append(RemoteDMATransfer(dst_ids=ids, dma_engine_mask=mask, remote_sem=T.sem[rsem],
+                                         srcs=[ap(src)], dsts=[ap(dst) for _ in dests], alu_op=0))
+            sent += _nbits(mask)
+        g.remote_dma_fused(trs, local_sem=T.sem.snt)
+
+    for slot, cnt, k in sorted(selfload.get(core, []), key=lambda s: -s[1]):
+        g.scalar.wait_ge(T.sem["rl%d" % slot], cnt)
+        g.scalar.dma_start(ap(("s", k)), T.wd[slot]).then_inc(T.sem["w%d" % k], 16)
+
+    if rank is not None:
+        ne = len(experts)
+        on = [1 if experts[j // tok] in route[rank][j % tok] else 0 for j in range(ne * tok)]
+        g.vector.memset(T.mask[:], 0.0).then_inc(T.sem.vs, 1)
+        g.vector.wait_ge(T.sem.vs, 1)
+        n, j = 1, 0
+        while j < len(on):
+            if on[j]:
+                a = j
+                while j < len(on) and on[j]:
+                    j += 1
+                g.vector.memset(T.mask[:, a:j], 1.0).then_inc(T.sem.vs, 1)
+                n += 1
+            else:
+                j += 1
+        g.vector.wait_ge(T.sem.vs, n)
+        g.vector.wait_ge(T.sem.xl, 16)
+        for k in range(ne):
+            g.vector.tensor_tensor(T.xm[:, k * tok:(k + 1) * tok], T.xsb[:], T.mask[:, k * tok:(k + 1) * tok],
+                                   AluOpType.mult).then_inc(T.sem.vm, 1)
+        g.tensor.wait_ge(T.sem.vm, ne)
+        order = sorted(range(ne), key=lambda k: (0 if experts[k] == rank else 1, k))
+        for i, k in enumerate(order):
+            g.tensor.wait_ge(T.sem["w%d" % k], expect[core][k])
+            mmi = g.tensor.matmul(T.ps[:], T.wsb[:, k * 128:(k + 1) * 128], T.xm[:, k * tok:(k + 1) * tok],
+                                  i == 0, i == ne - 1)
+        mmi.then_inc(T.sem.mm, 1)
+        g.vector.wait_ge(T.sem.mm, 1)
+        g.vector.tensor_copy(T.ysb[:], T.ps[:]).then_inc(T.sem.cp, 1)
+        g.sync.wait_ge(T.sem.cp, 1)
+        g.sync.dma_start(T.y[:], T.ysb[:]).then_inc(T.sem.st, 16)
+        g.sync.wait_ge(T.sem.st, 16)
+
+    if sent:
+        g.wait_ge(T.sem.snt, sent)

@@ -6,20 +6,47 @@ SCRATCH = {
     "wd": ("dram", [2, 128, 128], "bfloat16"),
     "wsb": ("sbuf", [128, 768], "bfloat16"),
     "xsb": ("sbuf", [128, 32], "bfloat16"),
-    "mask": ("sbuf", [128, 192], "bfloat16"),
+    "mask": ("sbuf", [128, 6, 32], "bfloat16"),
     "xm": ("sbuf", [128, 192], "bfloat16"),
     "ysb": ("sbuf", [128, 32], "bfloat16"),
     "ps": ("psum", [128, 32], "float32"),
 }
 SEMAPHORES = ["ld", "xl", "rl0", "rl1", "w0", "w1", "w2", "w3", "w4", "w5", "snt", "vs", "vm", "mm", "cp", "st"]
 
-INBOUND = {3: (202, 0), 13: (206, 0), 8: (195, 0), 10: (197, 1), 9: (199, 0)}
-FAR = {}
+INBOUND = {3: [(194, [196, 197, 198, 199])], 13: [(206, [196, 197]), (202, [198, 199])], 10: [(197, [196, 198, 199])],
+           8: [(195, [196, 197, 198, 199])], 9: [(199, [196, 197, 198])], 19: [(197, [])]}
+PAIRS = {8: [0, 5, 7], 9: [15, 11, 12]}
 _CACHE = {}
 
 
 def _nbits(m):
     return bin(m).count("1")
+
+
+def cover(route_r, experts, tok):
+    idx = {e: k for k, e in enumerate(experts)}
+    unc = set((idx[e], t) for t in range(tok) for e in route_r[t])
+    ne = len(experts)
+    esets = [(a,) for a in range(ne)] + [(a, b) for a in range(ne) for b in range(a + 1, ne)]
+    out = []
+    while unc:
+        best = None
+        for es in esets:
+            te = [t for t in range(tok) if all((k, t) in unc for k in es)]
+            s = set(te)
+            for t0 in te:
+                for step in range(1, tok):
+                    n = 1
+                    while t0 + n * step in s:
+                        n += 1
+                    if best is None or n * len(es) > best[0]:
+                        best = (n * len(es), es, t0, step, n)
+        _, es, t0, step, n = best
+        out.append((es[0], es[-1] + 1, max(1, es[-1] - es[0]), t0, t0 + (n - 1) * step + 1, step))
+        for k in es:
+            for i in range(n):
+                unc.discard((k, t0 + i * step))
+    return out
 
 
 def build_plan(cores, experts):
@@ -31,31 +58,40 @@ def build_plan(cores, experts):
     def place(c):
         return (topo.host(c), topo.chip(c))
 
+    def count_in(c, d):
+        inport[(place(c), d)] = inport.get((place(c), d), 0) + 1
+
     for k, e in enumerate(experts):
         root = cores[e]
         base = root - root % 8
+        mbase = base ^ 8
         par = topo.chip(root) % 2
         on_big = root in big
-        own = 1 if on_big else 0
-        wk = "w%d" % k
-        far = FAR.get(e, [])
-        covered = [c for _, ds in far for c in ds]
-        singles = [c for c in cores if c not in big and c != root and c not in covered]
+        ts = 1 if on_big else 0
+        rl, wk = "rl%d" % ts, "w%d" % k
+        send = {}
+        first = []
+        for rc, ds in INBOUND[e]:
+            send[rc] = list(ds)
+            first.append(rc)
+        for ch in PAIRS.get(e, []):
+            send[ch * 8 + 2] = [ch * 8 + 6, (ch ^ 1) * 8 + 6]
+            count_in(ch * 8 + 6, 0)
+        done = [c for ds in send.values() for c in ds]
+        singles = [c for c in cores if c not in big and c != root and c not in done]
         same = [c for c in singles if topo.chip(c) % 2 == par]
         cross = [c for c in singles if topo.chip(c) % 2 != par]
+        caps_same = {1: [(base + 0, 2), (base + 1, 2)], 0: [(base + 4, 2), (base + (6 if on_big else 5), 2)]}
         if on_big:
-            caps_same = {1: [(base + 0, 3), (base + 1, 2)], 0: [(base + 4, 3)]}
-            caps_cross = {1: [(base + 2, 3)], 0: [(base + 6, 3), (root, 2)]}
-        elif far:
-            caps_same = {1: [(base + 0, 2), (base + 1, 2)], 0: [(base + 4, 2), (base + 5, 2)]}
+            caps_cross = {1: [(mbase + 0, 2), (mbase + 1, 2)], 0: [(mbase + 4, 2), (mbase + 5, 2)]}
+        elif e in PAIRS:
             caps_cross = {1: [(base + 2, 2), (base + 3, 2)], 0: [(base + 7, 2)]}
         else:
-            caps_same = {1: [(base + 0, 2), (base + 1, 2)], 0: [(base + 4, 2), (base + 5, 2)]}
-            caps_cross = {1: [(base + 2, 2), (base + 3, 2)], 0: [(base + 7, 2), (root, 2)]}
-        send = {}
+            send[mbase + 4] = [mbase + 6]
+            cross = [c for c in cross if c != mbase + 6]
+            caps_cross = {1: [(base + 2, 2), (base + 3, 2)], 0: [(base + 7, 2), (mbase + 4, 1)]}
         for dests, caps in ((same, caps_same), (cross, caps_cross)):
-            cap1 = sum(n for _, n in caps[1])
-            n1 = cap1 if on_big else min(cap1, (len(dests) + 1) // 2)
+            n1 = min(sum(n for _, n in caps[1]), (len(dests) + 1) // 2)
             order = sorted(dests, key=lambda c: (inport.get((place(c), 1), 0) - inport.get((place(c), 0), 0), c))
             for d, part in ((1, order[:n1]), (0, order[n1:])):
                 names = [s for s, _ in caps[d]]
@@ -68,51 +104,36 @@ def build_plan(cores, experts):
                     left[s] -= 1
                     i += 1
                     send.setdefault(s, []).append(c)
-                    inport[(place(c), d)] = inport.get((place(c), d), 0) + 1
-        tr = []
-        helpers = [s for s in send if s != root]
+                    count_in(c, d)
         if on_big:
-            helpers = sorted(set(helpers) | set(c for c in big if c != root))
-        tr.append((0xFF00, "rl0", ("d", own), ("d", 0), sorted(helpers)))
-        direct = send.get(root, [])
-        bmask, dmask = (0x000F, 0x00F0) if direct and not on_big else (0x00FF, 0x00FF)
-        if not on_big:
-            rc, slot = INBOUND[e]
-            away = [rc] + [f for f, _ in far]
-            tr.append((bmask, "rl%d" % slot, ("d", own), ("d", slot), away))
-            targets = [c for c in big if c != rc]
-            m = 0xFFFF if place(rc) == place(big[0]) else 0x00FF
-            jobs.setdefault(rc, []).append((("rl%d" % slot, _nbits(bmask)), [(m, wk, ("d", slot), ("s", k), targets)]))
-            for c in targets:
-                expect.setdefault(c, {})[k] = _nbits(m)
-            if rc in big:
-                selfload.setdefault(rc, []).append((slot, _nbits(bmask), k))
-                expect.setdefault(rc, {})[k] = 16
-            for f, ds in far:
-                near = [c for c in ds if place(c) == place(f)]
-                off = [c for c in ds if place(c) != place(f)]
-                ftr = [(0x00FF, wk, ("d", slot), ("s", k), off)]
-                if near:
-                    ftr.append((0xFF00, wk, ("d", slot), ("s", k), near))
-                jobs.setdefault(f, []).append((("rl%d" % slot, _nbits(bmask)), ftr))
-                for c in ds:
-                    expect.setdefault(c, {})[k] = 8
-                    if place(c) != place(f):
-                        inport[(place(c), topo.die(f))] = inport.get((place(c), topo.die(f)), 0) + 1
-        if direct:
-            tr.append((dmask, wk, ("d", own), ("s", k), direct))
-        for c in direct:
-            expect.setdefault(c, {})[k] = _nbits(dmask)
-        jobs.setdefault(root, []).insert(0, (("ld", 16), tr))
+            for c in big:
+                if c != root:
+                    send.setdefault(c, [])
+        near = sorted(s for s in send if place(s) == place(root))
+        away = [s for s in send if place(s) != place(root)]
+        if e in PAIRS:
+            groups = [(0xFF00, near), (0x000F, [s for s in away if s in first]), (0x00F0, [s for s in away if s not in first])]
+        else:
+            groups = [(0xFF00, near), (0x00FF, away)]
+        jobs[root] = [(("ld", 16), [(m, rl, ("d", ts), ("d", ts), us) for m, us in groups if us])] + jobs.get(root, [])
         expect.setdefault(root, {})[k] = 16
-        for s in helpers:
-            if s in send:
-                jobs.setdefault(s, []).insert(0, (("rl0", 8), [(0x00FF, wk, ("d", 0), ("s", k), send[s])]))
-                for c in send[s]:
-                    expect.setdefault(c, {})[k] = 8
-            if s in big:
-                selfload.setdefault(s, []).append((0, 8, k))
-                expect.setdefault(s, {})[k] = 16
+        for m, us in groups:
+            for s in us:
+                off = [c for c in send[s] if place(c) != place(s)]
+                home = [c for c in send[s] if place(c) == place(s)]
+                tr = []
+                if off:
+                    tr.append((0x00FF, wk, ("d", ts), ("s", k), off))
+                if home:
+                    tr.append((0xFF00 if off else 0xFFFF, wk, ("d", ts), ("s", k), home))
+                for mm, _, _, _, ds in tr:
+                    for c in ds:
+                        expect.setdefault(c, {})[k] = _nbits(mm)
+                if tr:
+                    jobs.setdefault(s, []).append(((rl, _nbits(m)), tr))
+                if s in cores:
+                    selfload.setdefault(s, []).append((ts, _nbits(m), k))
+                    expect.setdefault(s, {})[k] = 16
     return jobs, selfload, expect
 
 
@@ -153,29 +174,23 @@ def rank_program(g, core, T, topo):
             sent += _nbits(mask)
         g.remote_dma_fused(trs, local_sem=T.sem.snt)
 
-    for slot, cnt, k in sorted(selfload.get(core, []), key=lambda s: -s[1]):
-        g.scalar.wait_ge(T.sem["rl%d" % slot], cnt)
-        g.scalar.dma_start(ap(("s", k)), T.wd[slot]).then_inc(T.sem["w%d" % k], 16)
+    for i, (slot, cnt, k) in enumerate(selfload.get(core, [])):
+        q = g.scalar if i % 2 == 0 else g.sync
+        q.wait_ge(T.sem["rl%d" % slot], cnt)
+        q.dma_start(ap(("s", k)), T.wd[slot]).then_inc(T.sem["w%d" % k], 16)
 
     if rank is not None:
         ne = len(experts)
-        on = [1 if experts[j // tok] in route[rank][j % tok] else 0 for j in range(ne * tok)]
         g.vector.memset(T.mask[:], 0.0).then_inc(T.sem.vs, 1)
         g.vector.wait_ge(T.sem.vs, 1)
-        n, j = 1, 0
-        while j < len(on):
-            if on[j]:
-                a = j
-                while j < len(on) and on[j]:
-                    j += 1
-                g.vector.memset(T.mask[:, a:j], 1.0).then_inc(T.sem.vs, 1)
-                n += 1
-            else:
-                j += 1
+        n = 1
+        for k0, k1, ks, t0, t1, ts in cover(route[rank], experts, tok):
+            g.vector.memset(T.mask[:, k0:k1:ks, t0:t1:ts], 1.0).then_inc(T.sem.vs, 1)
+            n += 1
         g.vector.wait_ge(T.sem.vs, n)
         g.vector.wait_ge(T.sem.xl, 16)
         for k in range(ne):
-            g.vector.tensor_tensor(T.xm[:, k * tok:(k + 1) * tok], T.xsb[:], T.mask[:, k * tok:(k + 1) * tok],
+            g.vector.tensor_tensor(T.xm[:, k * tok:(k + 1) * tok], T.xsb[:], T.mask[:, k, :],
                                    AluOpType.mult).then_inc(T.sem.vm, 1)
         g.tensor.wait_ge(T.sem.vm, ne)
         order = sorted(range(ne), key=lambda k: (0 if experts[k] == rank else 1, k))

from concourse.bass import DstId, RemoteDMATransfer
from concourse.mybir import dt, AluOpType
import comms_topo

SCRATCH = {
    "wd": ("dram", [2, 128, 128], "bfloat16"),
    "wsb": ("sbuf", [128, 768], "bfloat16"),
    "xsb": ("sbuf", [128, 32], "bfloat16"),
    "mask": ("sbuf", [128, 6, 32], "bfloat16"),
    "xm": ("sbuf", [128, 192], "bfloat16"),
    "ysb": ("sbuf", [128, 32], "bfloat16"),
    "ps": ("psum", [128, 32], "float32"),
}
SEMAPHORES = ["ld", "xl", "rl0", "rl1", "w0", "w1", "w2", "w3", "w4", "w5", "snt", "vs", "vm", "mm", "cp", "st"]

INBOUND = {3: [(194, [196, 197, 198, 199])], 13: [(206, [196, 197]), (202, [198, 199])], 10: [(197, [196, 198, 199])],
           8: [(195, [196, 197, 198, 199])], 9: [(199, [196, 197, 198])], 19: [(197, [])]}
PAIRS = {8: [0, 5, 7], 9: [15, 11, 12]}
_CACHE = {}


def _nbits(m):
    return bin(m).count("1")


def cover(route_r, experts, tok):
    idx = {e: k for k, e in enumerate(experts)}
    unc = set((idx[e], t) for t in range(tok) for e in route_r[t])
    ne = len(experts)
    esets = [(a,) for a in range(ne)] + [(a, b) for a in range(ne) for b in range(a + 1, ne)]
    out = []
    while unc:
        best = None
        for es in esets:
            te = [t for t in range(tok) if all((k, t) in unc for k in es)]
            s = set(te)
            for t0 in te:
                for step in range(1, tok):
                    n = 1
                    while t0 + n * step in s:
                        n += 1
                    if best is None or n * len(es) > best[0]:
                        best = (n * len(es), es, t0, step, n)
        _, es, t0, step, n = best
        out.append((es[0], es[-1] + 1, max(1, es[-1] - es[0]), t0, t0 + (n - 1) * step + 1, step))
        for k in es:
            for i in range(n):
                unc.discard((k, t0 + i * step))
    return out


def build_plan(cores, experts):
    topo = comms_topo
    jobs, selfload, expect = {}, {}, {}
    inport = {}
    big = [c for c in cores if topo.host(c) == 1]

    def place(c):
        return (topo.host(c), topo.chip(c))

    def count_in(c, d):
        inport[(place(c), d)] = inport.get((place(c), d), 0) + 1

    for k, e in enumerate(experts):
        root = cores[e]
        base = root - root % 8
        mbase = base ^ 8
        par = topo.chip(root) % 2
        on_big = root in big
        ts = 1 if on_big else 0
        rl, wk = "rl%d" % ts, "w%d" % k
        send = {}
        first = []
        for rc, ds in INBOUND[e]:
            send[rc] = list(ds)
            first.append(rc)
        for ch in PAIRS.get(e, []):
            send[ch * 8 + 2] = [ch * 8 + 6, (ch ^ 1) * 8 + 6]
            count_in(ch * 8 + 6, 0)
        done = [c for ds in send.values() for c in ds]
        singles = [c for c in cores if c not in big and c != root and c not in done]
        same = [c for c in singles if topo.chip(c) % 2 == par]
        cross = [c for c in singles if topo.chip(c) % 2 != par]
        caps_same = {1: [(base + 0, 2), (base + 1, 2)], 0: [(base + 4, 2), (base + (6 if on_big else 5), 2)]}
        if on_big:
            caps_cross = {1: [(mbase + 0, 2), (mbase + 1, 2)], 0: [(mbase + 4, 2), (mbase + 5, 2)]}
        elif e in PAIRS:
            caps_cross = {1: [(base + 2, 2), (base + 3, 2)], 0: [(base + 7, 2)]}
        else:
            send[mbase + 4] = [mbase + 6]
            cross = [c for c in cross if c != mbase + 6]
            caps_cross = {1: [(base + 2, 2), (base + 3, 2)], 0: [(base + 7, 2), (mbase + 4, 1)]}
        for dests, caps in ((same, caps_same), (cross, caps_cross)):
            n1 = min(sum(n for _, n in caps[1]), (len(dests) + 1) // 2)
            order = sorted(dests, key=lambda c: (inport.get((place(c), 1), 0) - inport.get((place(c), 0), 0), c))
            for d, part in ((1, order[:n1]), (0, order[n1:])):
                names = [s for s, _ in caps[d]]
                left = dict(caps[d])
                i = 0
                for c in part:
                    while left[names[i % len(names)]] == 0:
                        i += 1
                    s = names[i % len(names)]
                    left[s] -= 1
                    i += 1
                    send.setdefault(s, []).append(c)
                    count_in(c, d)
        if on_big:
            for c in big:
                if c != root:
                    send.setdefault(c, [])
        near = sorted(s for s in send if place(s) == place(root))
        away = [s for s in send if place(s) != place(root)]
        if e in PAIRS:
            groups = [(0xFF00, near), (0x000F, [s for s in away if s in first]), (0x00F0, [s for s in away if s not in first])]
        else:
            groups = [(0xFF00, near), (0x00FF, away)]
        jobs[root] = [(("ld", 16), [(m, rl, ("d", ts), ("d", ts), us) for m, us in groups if us])] + jobs.get(root, [])
        expect.setdefault(root, {})[k] = 16
        for m, us in groups:
            for s in us:
                off = [c for c in send[s] if place(c) != place(s)]
                home = [c for c in send[s] if place(c) == place(s)]
                tr = []
                if off:
                    tr.append((0x00FF, wk, ("d", ts), ("s", k), off))
                if home:
                    tr.append((0xFF00 if off else 0xFFFF, wk, ("d", ts), ("s", k), home))
                for mm, _, _, _, ds in tr:
                    for c in ds:
                        expect.setdefault(c, {})[k] = _nbits(mm)
                if tr:
                    jobs.setdefault(s, []).append(((rl, _nbits(m)), tr))
                if s in cores:
                    selfload.setdefault(s, []).append((ts, _nbits(m), k))
                    expect.setdefault(s, {})[k] = 16
    return jobs, selfload, expect


def rank_program(g, core, T, topo):
    cores = list(T.cores)
    experts = list(T.tables["EXPERTS"])
    route = T.tables["ROUTE"]
    tok = T.tables["TOK"]
    if "p" not in _CACHE:
        _CACHE["p"] = build_plan(cores, experts)
    jobs, selfload, expect = _CACHE["p"]
    rank = T.rank_of(core)
    is_root = rank is not None and rank in experts

    def ap(where):
        kind, i = where
        return T.wd[i] if kind == "d" else T.wsb[:, i * 128:(i + 1) * 128]

    if is_root:
        k_own = experts.index(rank)
        g.sync.dma_start(T.wd[1 if topo.host(core) == 1 else 0], T.w[:]).then_inc(T.sem.ld, 16)
    if rank is not None:
        g.scalar.dma_start(T.xsb[:], T.x[:]).then_inc(T.sem.xl, 16)
    if is_root:
        g.scalar.dma_start(ap(("s", k_own)), T.w[:]).then_inc(T.sem["w%d" % k_own], 16)

    sent = 0
    for wait, transfers in jobs.get(core, []):
        g.wait_ge(T.sem[wait[0]], wait[1])
        trs = []
        for mask, rsem, src, dst, dests in transfers:
            ids = []
            for d in dests:
                rid, pid = topo.addr(d, core)
                ids.append(DstId(rid=rid, pnc=pid))
            trs.append(RemoteDMATransfer(dst_ids=ids, dma_engine_mask=mask, remote_sem=T.sem[rsem],
                                         srcs=[ap(src)], dsts=[ap(dst) for _ in dests], alu_op=0))
            sent += _nbits(mask)
        g.remote_dma_fused(trs, local_sem=T.sem.snt)

    for i, (slot, cnt, k) in enumerate(selfload.get(core, [])):
        q = g.scalar if i % 2 == 0 else g.sync
        q.wait_ge(T.sem["rl%d" % slot], cnt)
        q.dma_start(ap(("s", k)), T.wd[slot]).then_inc(T.sem["w%d" % k], 16)

    if rank is not None:
        ne = len(experts)
        g.vector.memset(T.mask[:], 0.0).then_inc(T.sem.vs, 1)
        g.vector.wait_ge(T.sem.vs, 1)
        n = 1
        for k0, k1, ks, t0, t1, ts in cover(route[rank], experts, tok):
            g.vector.memset(T.mask[:, k0:k1:ks, t0:t1:ts], 1.0).then_inc(T.sem.vs, 1)
            n += 1
        g.vector.wait_ge(T.sem.vs, n)
        g.vector.wait_ge(T.sem.xl, 16)
        for k in range(ne):
            g.vector.tensor_tensor(T.xm[:, k * tok:(k + 1) * tok], T.xsb[:], T.mask[:, k, :],
                                   AluOpType.mult).then_inc(T.sem.vm, 1)
        g.tensor.wait_ge(T.sem.vm, ne)
        order = sorted(range(ne), key=lambda k: (0 if experts[k] == rank else 1, k))
        for i, k in enumerate(order):
            g.tensor.wait_ge(T.sem["w%d" % k], expect[core][k])
            mmi = g.tensor.matmul(T.ps[:], T.wsb[:, k * 128:(k + 1) * 128], T.xm[:, k * tok:(k + 1) * tok],
                                  i == 0, i == ne - 1)
        mmi.then_inc(T.sem.mm, 1)
        g.vector.wait_ge(T.sem.mm, 1)
        g.vector.tensor_copy(T.ysb[:], T.ps[:]).then_inc(T.sem.cp, 1)
        g.sync.wait_ge(T.sem.cp, 1)
        g.sync.dma_start(T.y[:], T.ysb[:]).then_inc(T.sem.st, 16)
        g.sync.wait_ge(T.sem.st, 16)

    if sent:
        g.wait_ge(T.sem.snt, sent)
